import numpy as np
import ml_dtypes


def mxq(x, axis, fmt="e4m3"):
    dtype, down = {"e4m3": (ml_dtypes.float8_e4m3fn, 7), "e5m2": (ml_dtypes.float8_e5m2, 14)}[fmt]
    v = np.moveaxis(np.asarray(x, np.float32).astype(ml_dtypes.bfloat16).astype(np.float64), axis, -1)
    blocks = v.reshape(v.shape[:-1] + (-1, 32))
    amax = np.abs(blocks).max(-1, keepdims=True)
    byte = np.maximum(np.where(amax > 0, np.frexp(amax)[1] - 1 + 127, 0) - down, 1)
    scale = np.exp2(byte - 127.0)
    codes = (blocks / scale).astype(np.float32).astype(dtype).astype(np.float64)
    return np.moveaxis((codes * scale).reshape(v.shape), -1, axis)


WIDE = False


def mx_kscale(k):
    if not WIDE:
        return np.ones(k)
    levels = np.array([10, -10, 5, -5, 0])
    if k % 512:
        return np.exp2(np.random.permutation(np.resize(levels, k // 32))).repeat(32)
    a = np.empty((k // 512, 16))
    for p in range(k // 512):
        a[p, :8] = np.random.permutation(np.resize(levels, 8))
        for g in range(8):
            far = levels[np.abs(levels - a[p, g]) >= 10]
            a[p, g + 8] = far[np.random.randint(len(far))]
    return np.exp2(a.ravel()).repeat(32)


def f64(x):
    return np.asarray(x).astype(np.float64)


def striped(idx):
    return np.tile(idx.reshape(-1, 16).T, (8, 1)).astype(np.uint16)


def unstriped(offs):
    return offs[:16].T.reshape(-1).astype(np.int64)


def gelu(v):
    return 0.5 * v * (1.0 + np.tanh(np.sqrt(2.0 / np.pi) * (v + 0.044715 * v**3)))


K, T, E, C, H, N = 512, 512, 4, 128, 512, 128


def by_expert(wq, xq):
    return np.concatenate([wq[e].T @ xq[:, e * C:(e + 1) * C] for e in range(E)], axis=1)


def setup_inputs():
    n = np.random.standard_normal
    s = mx_kscale(K)[:, None]
    u = mx_kscale(H)
    return {
        "xT": (n((K, T)) * s).astype(np.float32),
        "w1": (n((E + 1, K, H)) / np.sqrt(K) / s[None]).astype(np.float32),
        "w3": (n((E + 1, K, H)) / np.sqrt(K) / s[None] * u[None, None, :]).astype(np.float32),
        "w2": (n((E + 1, H, N)) / np.sqrt(H) / u[None, :, None]).astype(np.float32),
        "gate": np.tile(np.random.uniform(0.2, 1.0, E * C), (N, 1)).astype(np.float32),
        "offs": striped(np.random.permutation(T)[:E * C]),
    }


def reference(xT, w1, w3, w2, gate, offs):
    idx = unstriped(offs)
    w1q, w3q, w2q = mxq(f64(w1), 1, "e4m3"), mxq(f64(w3), 1, "e4m3"), mxq(f64(w2), 1, "e4m3")
    xs = mxq(f64(xT), 0, "e4m3")
    hs = gelu(w1q[E].T @ xs) * (w3q[E].T @ xs)
    ys = w2q[E].T @ mxq(hs, 0, "e4m3")
    xq = mxq(f64(xT)[:, idx], 0, "e4m3")
    h = gelu(by_expert(w1q, xq))
    h = h * by_expert(w3q, xq)
    y = by_expert(w2q, mxq(h, 0, "e4m3"))
    out = ys
    out[:, idx] += f64(gate) * y
    return out

@@ -1,0 +1,257 @@
+from contextlib import ExitStack
+
+import concourse.mybir as mybir
+
+K, T, E, C, H, N = 512, 512, 4, 128, 512, 128
+FLOPS = 2 * (2 * T) * (2 * K * H + H * N)
+
+F32 = mybir.dt.float32
+BF16 = mybir.dt.bfloat16
+U32 = mybir.dt.uint32
+U16 = mybir.dt.uint16
+U8 = mybir.dt.uint8
+FP8X4 = mybir.dt.float8_e4m3fn_x4
+GELU = mybir.ActivationFunctionType.Gelu_apprx_tanh
+MULT = mybir.AluOpType.mult
+ADD = mybir.AluOpType.add
+
+P = 128
+PACK = 4
+SHARED = E
+
+
+def tile_moe_shr_glu_gelu_kernel(tc, xT, w1, w3, w2, gate, offs, out):
+    nc = tc.nc
+    with ExitStack() as ctx:
+        keep = ctx.enter_context(tc.tile_pool(name="keep", bufs=1))
+        work = ctx.enter_context(tc.tile_pool(name="work", bufs=4))
+        psum = ctx.enter_context(tc.psum_pool(name="psum", bufs=1))
+
+        offsets = keep.tile([P, T // 16], U16, name="offsets")
+        x_raw = [keep.tile([P, 2, T], F32, name=f"x_raw{u}") for u in range(2)]
+        w_raw = {}
+        x_rows = xT.rearrange("(p u h) t -> p u h t", u=2, h=2)
+        nc.sync.dma_start(x_raw[0][:], x_rows[:, 0])
+        nc.sync.dma_start(offsets[:], offs)
+        nc.sync.dma_start(x_raw[1][:], x_rows[:, 1])
+
+        def load(name, src, e):
+            raw = keep.tile([P, PACK, src.shape[2]], F32, name=f"{name}_raw{e}")
+            nc.sync.dma_start(raw[:], src[e].rearrange("(p j) c -> p j c", j=PACK))
+            w_raw[name, e] = raw
+
+        load("w1", w1, SHARED)
+        load("w3", w3, SHARED)
+        load("w2", w2, SHARED)
+        gates = keep.tile([P, T], F32, name="gates")
+        for e in range(E):
+            load("w1", w1, e)
+            load("w3", w3, e)
+            load("w2", w2, e)
+            if e == 0:
+                nc.sync.dma_start(gates[:], gate)
+
+        tiny = keep.tile([P, 2], F32, name="tiny")
+        nc.gpsimd.memset(tiny[:], 0.0)
+        nc.scalar.activation(tiny[:, 1:2], tiny[:, 0:1], GELU)
+
+        x_pairs = [keep.tile([P, T, 2], BF16, name=f"x_pairs{u}", align_bytes=64) for u in range(2)]
+        x_slots = keep.tile([P, T, PACK], BF16, name="x_slots", align_bytes=64)
+        x_words = x_slots[:].rearrange("p s j -> p (s j)").bitcast(U32).rearrange("p (s u) -> p s u", u=2)
+        x_codes = keep.tile([P, T], U32, name="x_codes", align_bytes=64)
+        x_scales = keep.tile([P, T], U8, name="x_scales", align_bytes=64)
+        nc.vector.tensor_copy(x_pairs[0][:], x_raw[0][:].rearrange("p h t -> p t h"))
+        nc.scalar.copy(x_pairs[1][:], x_raw[1][:].rearrange("p h t -> p t h"))
+        HALF = T // 2
+        for u in range(2):
+            window = x_pairs[u][:].rearrange("p t h -> p (t h)").bitcast(U32)
+            for s in range(2):
+                nc.vector.tensor_copy(
+                    x_words[:, s * HALF : (s + 1) * HALF, u],
+                    window.indirect(offsets[:, s * HALF // 16 : (s + 1) * HALF // 16]),
+                )
+        nc.vector.quantize_mx(
+            out=x_codes[:].bitcast(FP8X4), scales=x_scales[:], in_=x_slots[:].rearrange("p s j -> p (s j)")
+        )
+
+        codes = {}
+        scales = {}
+        grouped = {}
+
+        def new_weight(name, e):
+            width = w_raw[name, e].shape[2]
+            grouped[name, e] = keep.tile([P, width * PACK], BF16, name=f"{name}_grouped{e}", align_bytes=64)
+            codes[name, e] = keep.tile([P, width], U32, name=f"{name}_codes{e}", align_bytes=64)
+            scales[name, e] = keep.tile([P, width], U8, name=f"{name}_scales{e}", align_bytes=64)
+
+        def cast_hidden(engine, name, e, lo, hi):
+            if lo == hi:
+                return
+            dst = grouped[name, e][:].rearrange("p (t m j) -> p m j t", t=PACK, j=PACK)
+            src = w_raw[name, e][:].rearrange("p j (m t) -> p m j t", t=PACK)
+            engine(dst[:, lo:hi], src[:, lo:hi])
+
+        def cast_out(engine, e):
+            dst = grouped["w2", e][:].rearrange("p (n j) -> p n j", j=PACK)
+            src = w_raw["w2", e][:].rearrange("p j n -> p n j")
+            engine(dst, src)
+
+        def quantize_weight(name, e):
+            nc.vector.quantize_mx(
+                out=codes[name, e][:].bitcast(FP8X4), scales=scales[name, e][:], in_=grouped[name, e][:]
+            )
+
+        gelus = {}
+        gated = {}
+        linear = {}
+        h_codes = {}
+        h_scales = {}
+
+        def hidden_product(acc, name, e, g):
+            for t in range(PACK):
+                cols = slice(t * P, (t + 1) * P)
+                slots = slice(g * C, (g + 1) * C)
+                nc.tensor.matmul_mx(
+                    out=acc[:, t, :],
+                    lhsT=codes[name, e][:, cols].bitcast(FP8X4),
+                    lhsT_scale=scales[name, e][:, cols],
+                    rhs=x_codes[:, slots].bitcast(FP8X4),
+                    rhs_scale=x_scales[:, slots],
+                    start=True,
+                    stop=True,
+                )
+
+        def first_layer_gelu(e, g):
+            acc = psum.tile([P, PACK, C], F32, name="gelu_acc", bufs=3)
+            hidden_product(acc, "w1", e, g)
+            gelus[e, g] = work.tile([P, C, PACK], F32, name="gelu")
+            nc.scalar.activation(gelus[e, g][:], acc[:].rearrange("p t s -> p s t"), GELU)
+
+        def first_layer_linear(e, g):
+            acc = psum.tile([P, PACK, C], F32, name="linear_acc", bufs=2)
+            hidden_product(acc, "w3", e, g)
+            linear[e, g] = acc
+
+        def gate_hidden(e, g):
+            gated[e, g] = work.tile([P, C, PACK], BF16, name="gated", align_bytes=64)
+            nc.vector.tensor_tensor(
+                gated[e, g][:], gelus[e, g][:], linear[e, g][:].rearrange("p t s -> p s t"), MULT
+            )
+
+        def quantize_hidden(e, g):
+            h_codes[e, g] = work.tile([P, C], U32, name="h_codes", align_bytes=64)
+            h_scales[e, g] = work.tile([P, C], U8, name="h_scales", align_bytes=64)
+            nc.vector.quantize_mx(
+                out=h_codes[e, g][:].bitcast(FP8X4),
+                scales=h_scales[e, g][:],
+                in_=gated[e, g][:].rearrange("p s t -> p (s t)"),
+            )
+
+        def second_layer(acc, e, g):
+            nc.tensor.matmul_mx(
+                out=acc,
+                lhsT=codes["w2", e][:].bitcast(FP8X4),
+                lhsT_scale=scales["w2", e][:],
+                rhs=h_codes[e, g][:].bitcast(FP8X4),
+                rhs_scale=h_scales[e, g][:],
+                start=True,
+                stop=True,
+            )
+
+        S1 = {SHARED: 96, 0: 96, 1: 96, 2: 96, 3: 96}
+        S3 = {SHARED: 56, 0: 72, 1: 72, 2: 72, 3: 64}
+
+        def prepare_first(e):
+            new_weight("w1", e)
+            cast_hidden(nc.scalar.copy, "w1", e, 0, S1[e])
+            cast_hidden(nc.vector.tensor_copy, "w1", e, S1[e], P)
+
+        def prepare_second(e):
+            new_weight("w3", e)
+            cast_hidden(nc.scalar.copy, "w3", e, 0, S3[e])
+            cast_hidden(nc.vector.tensor_copy, "w3", e, S3[e], P)
+
+        def prepare_out(e, engine):
+            new_weight("w2", e)
+            cast_out(engine, e)
+
+        shared_acc = psum.tile([P, T], F32, name="shared_acc")
+        result = keep.tile([P, T], F32, name="result")
+        routed_acc = {}
+        weighted = {}
+        total = {}
+
+        def shared_out(g):
+            second_layer(shared_acc[:, g * C : (g + 1) * C], SHARED, g)
+
+        def route(e):
+            routed_acc[e] = psum.tile([P, C], F32, name="routed_acc", bufs=2)
+            second_layer(routed_acc[e][:], e, e)
+
+        def weigh(e):
+            weighted[e] = work.tile([P, C], F32, name="weighted")
+            nc.vector.tensor_tensor(weighted[e][:], routed_acc[e][:], gates[:, e * C : (e + 1) * C], MULT)
+
+        def add_shared(e):
+            total[e] = work.tile([P, C], F32, name="total")
+            nc.vector.tensor_tensor(total[e][:], weighted[e][:], shared_acc[:, e * C : (e + 1) * C], ADD)
+
+        def scatter(e):
+            nc.vector.tensor_copy(
+                result[:].indirect(offsets[:, e * C // 16 : (e + 1) * C // 16]), total[e][:]
+            )
+
+        prepare_first(SHARED)
+        quantize_weight("w1", SHARED)
+        prepare_second(SHARED)
+        first_layer_gelu(SHARED, 0)
+        first_layer_gelu(SHARED, 1)
+        first_layer_gelu(SHARED, 2)
+        quantize_weight("w3", SHARED)
+        first_layer_linear(SHARED, 0)
+        first_layer_linear(SHARED, 1)
+        prepare_out(SHARED, nc.vector.tensor_copy)
+        gate_hidden(SHARED, 0)
+        first_layer_linear(SHARED, 2)
+        prepare_first(0)
+        first_layer_gelu(SHARED, 3)
+        gate_hidden(SHARED, 1)
+        first_layer_linear(SHARED, 3)
+        quantize_hidden(SHARED, 0)
+        quantize_weight("w2", SHARED)
+        gate_hidden(SHARED, 2)
+        quantize_hidden(SHARED, 1)
+        gate_hidden(SHARED, 3)
+        quantize_hidden(SHARED, 2)
+        shared_out(0)
+        shared_out(1)
+        shared_out(2)
+
+        for e in range(E):
+            last = (e - 1, e - 1) if e else (SHARED, E - 1)
+            quantize_weight("w1", e)
+            quantize_hidden(*last)
+            prepare_second(e)
+            first_layer_gelu(e, e)
+            if e:
+                route(e - 1)
+                weigh(e - 1)
+            else:
+                shared_out(E - 1)
+            prepare_out(e, nc.scalar.copy)
+            quantize_weight("w3", e)
+            first_layer_linear(e, e)
+            if e:
+                add_shared(e - 1)
+            if e < E - 1:
+                prepare_first(e + 1)
+            quantize_weight("w2", e)
+            gate_hidden(e, e)
+            if e:
+                scatter(e - 1)
+        quantize_hidden(E - 1, E - 1)
+        route(E - 1)
+        weigh(E - 1)
+        add_shared(E - 1)
+        scatter(E - 1)
+        nc.sync.dma_start(out, result[:])

@@ -18,6 +18,7 @@ ADD = mybir.AluOpType.add
 P = 128
 PACK = 4
 SHARED = E
+HALF = T // 2
 
 
 def tile_moe_shr_glu_gelu_kernel(tc, xT, w1, w3, w2, gate, offs, out):
@@ -29,27 +30,39 @@ def tile_moe_shr_glu_gelu_kernel(tc, xT, w1, w3, w2, gate, offs, out):
 
         offsets = keep.tile([P, T // 16], U16, name="offsets")
         x_raw = [keep.tile([P, 2, T], F32, name=f"x_raw{u}") for u in range(2)]
-        w_raw = {}
         x_rows = xT.rearrange("(p u h) t -> p u h t", u=2, h=2)
         nc.sync.dma_start(x_raw[0][:], x_rows[:, 0])
         nc.sync.dma_start(offsets[:], offs)
         nc.sync.dma_start(x_raw[1][:], x_rows[:, 1])
 
+        w_raw = {}
+
         def load(name, src, e):
-            raw = keep.tile([P, PACK, src.shape[2]], F32, name=f"{name}_raw{e}")
+            raw = keep.tile([P, PACK, src.shape[2]], F32, name=f"{name}_raw{e}", tag=f"{name}_raw{e}")
             nc.sync.dma_start(raw[:], src[e].rearrange("(p j) c -> p j c", j=PACK))
             w_raw[name, e] = raw
 
+        w2_raw = {}
+
+        def load_w2(key, lo, hi):
+            w2_raw[key] = keep.tile([P, hi - lo, PACK * N], F32, name=f"w2_raw{key}")
+            nc.sync.dma_start(w2_raw[key][:], w2[lo:hi].rearrange("e (p j) n -> p e (j n)", j=PACK))
+
+        gates = keep.tile([P, T], F32, name="gates")
         load("w1", w1, SHARED)
         load("w3", w3, SHARED)
-        load("w2", w2, SHARED)
-        gates = keep.tile([P, T], F32, name="gates")
-        for e in range(E):
-            load("w1", w1, e)
-            load("w3", w3, e)
-            load("w2", w2, e)
-            if e == 0:
-                nc.sync.dma_start(gates[:], gate)
+        load("w1", w1, 0)
+        load_w2(2, SHARED, SHARED + 1)
+        load("w3", w3, 0)
+        load("w1", w1, 1)
+        load("w3", w3, 1)
+        load_w2(0, 0, 2)
+        nc.sync.dma_start(gates[:], gate)
+        load("w1", w1, 2)
+        load("w3", w3, 2)
+        load("w1", w1, 3)
+        load("w3", w3, 3)
+        load_w2(1, 2, 4)
 
         tiny = keep.tile([P, 2], F32, name="tiny")
         nc.gpsimd.memset(tiny[:], 0.0)
@@ -60,9 +73,12 @@ def tile_moe_shr_glu_gelu_kernel(tc, xT, w1, w3, w2, gate, offs, out):
         x_words = x_slots[:].rearrange("p s j -> p (s j)").bitcast(U32).rearrange("p (s u) -> p s u", u=2)
         x_codes = keep.tile([P, T], U32, name="x_codes", align_bytes=64)
         x_scales = keep.tile([P, T], U8, name="x_scales", align_bytes=64)
-        nc.vector.tensor_copy(x_pairs[0][:], x_raw[0][:].rearrange("p h t -> p t h"))
-        nc.scalar.copy(x_pairs[1][:], x_raw[1][:].rearrange("p h t -> p t h"))
-        HALF = T // 2
+        XS = 0
+        x_view = [r[:].rearrange("p h t -> p t h") for r in x_raw]
+        nc.vector.tensor_copy(x_pairs[0][:, XS:], x_view[0][:, XS:])
+        if XS:
+            nc.scalar.copy(x_pairs[0][:, :XS], x_view[0][:, :XS])
+        nc.scalar.copy(x_pairs[1][:], x_view[1])
         for u in range(2):
             window = x_pairs[u][:].rearrange("p t h -> p (t h)").bitcast(U32)
             for s in range(2):
@@ -77,9 +93,10 @@ def tile_moe_shr_glu_gelu_kernel(tc, xT, w1, w3, w2, gate, offs, out):
         codes = {}
         scales = {}
         grouped = {}
+        S1 = {SHARED: 96, 0: 80, 1: 80, 2: 80, 3: 88}
+        S3 = {SHARED: 64, 0: 88, 1: 88, 2: 88, 3: 72}
 
-        def new_weight(name, e):
-            width = w_raw[name, e].shape[2]
+        def new_weight(name, e, width):
             grouped[name, e] = keep.tile([P, width * PACK], BF16, name=f"{name}_grouped{e}", align_bytes=64)
             codes[name, e] = keep.tile([P, width], U32, name=f"{name}_codes{e}", align_bytes=64)
             scales[name, e] = keep.tile([P, width], U8, name=f"{name}_scales{e}", align_bytes=64)
@@ -91,19 +108,29 @@ def tile_moe_shr_glu_gelu_kernel(tc, xT, w1, w3, w2, gate, offs, out):
             src = w_raw[name, e][:].rearrange("p j (m t) -> p m j t", t=PACK)
             engine(dst[:, lo:hi], src[:, lo:hi])
 
-        def cast_out(engine, e):
-            dst = grouped["w2", e][:].rearrange("p (n j) -> p n j", j=PACK)
-            src = w_raw["w2", e][:].rearrange("p j n -> p n j")
-            engine(dst, src)
+        def prepare(name, e):
+            new_weight(name, e, H)
+            split = (S1 if name == "w1" else S3)[e]
+            cast_hidden(nc.scalar.copy, name, e, 0, split)
+            cast_hidden(nc.vector.tensor_copy, name, e, split, P)
+
+        def prepare_out(engine, key):
+            width = w2_raw[key].shape[1] * N
+            new_weight("w2", key, width)
+            engine(
+                grouped["w2", key][:].rearrange("p (e n j) -> p e n j", n=N, j=PACK),
+                w2_raw[key][:].rearrange("p e (j n) -> p e n j", j=PACK),
+            )
 
         def quantize_weight(name, e):
             nc.vector.quantize_mx(
                 out=codes[name, e][:].bitcast(FP8X4), scales=scales[name, e][:], in_=grouped[name, e][:]
             )
 
+        gelu_in = {}
         gelus = {}
-        gated = {}
         linear = {}
+        gated = {}
         h_codes = {}
         h_scales = {}
 
@@ -121,59 +148,56 @@ def tile_moe_shr_glu_gelu_kernel(tc, xT, w1, w3, w2, gate, offs, out):
                     stop=True,
                 )
 
-        def first_layer_gelu(e, g):
-            acc = psum.tile([P, PACK, C], F32, name="gelu_acc", bufs=3)
-            hidden_product(acc, "w1", e, g)
-            gelus[e, g] = work.tile([P, C, PACK], F32, name="gelu")
-            nc.scalar.activation(gelus[e, g][:], acc[:].rearrange("p t s -> p s t"), GELU)
+        def mm_gelu(e, g):
+            gelu_in[e, g] = psum.tile([P, PACK, C], F32, name="gelu_acc", bufs=3)
+            hidden_product(gelu_in[e, g], "w1", e, g)
 
-        def first_layer_linear(e, g):
-            acc = psum.tile([P, PACK, C], F32, name="linear_acc", bufs=2)
-            hidden_product(acc, "w3", e, g)
-            linear[e, g] = acc
+        def new_gelu(*units, tag):
+            tile = keep.tile([P, len(units) * C, PACK], F32, name=f"gelu_{tag}", tag=tag)
+            for i, unit in enumerate(units):
+                gelus[unit] = tile[:, i * C : (i + 1) * C]
+
+        def apply_gelu(e, g):
+            nc.scalar.activation(gelus[e, g], gelu_in[e, g][:].rearrange("p t s -> p s t"), GELU)
+
+        def mm_linear(e, g):
+            linear[e, g] = psum.tile([P, PACK, C], F32, name="linear_acc", bufs=2)
+            hidden_product(linear[e, g], "w3", e, g)
+
+        def new_hidden(*units):
+            width = len(units) * C
+            tile = work.tile([P, width, PACK], BF16, name="gated", align_bytes=64)
+            c = work.tile([P, width], U32, name="h_codes", align_bytes=64)
+            s = work.tile([P, width], U8, name="h_scales", align_bytes=64)
+            for i, unit in enumerate(units):
+                gated[unit] = tile[:, i * C : (i + 1) * C]
+                h_codes[unit] = c[:, i * C : (i + 1) * C]
+                h_scales[unit] = s[:, i * C : (i + 1) * C]
+            return tile, c, s
 
         def gate_hidden(e, g):
-            gated[e, g] = work.tile([P, C, PACK], BF16, name="gated", align_bytes=64)
             nc.vector.tensor_tensor(
-                gated[e, g][:], gelus[e, g][:], linear[e, g][:].rearrange("p t s -> p s t"), MULT
+                gated[e, g], gelus[e, g], linear[e, g][:].rearrange("p t s -> p s t"), MULT
             )
 
-        def quantize_hidden(e, g):
-            h_codes[e, g] = work.tile([P, C], U32, name="h_codes", align_bytes=64)
-            h_scales[e, g] = work.tile([P, C], U8, name="h_scales", align_bytes=64)
+        def quantize_hidden(h):
+            tile, c, s = h
             nc.vector.quantize_mx(
-                out=h_codes[e, g][:].bitcast(FP8X4),
-                scales=h_scales[e, g][:],
-                in_=gated[e, g][:].rearrange("p s t -> p (s t)"),
+                out=c[:].bitcast(FP8X4), scales=s[:], in_=tile[:].rearrange("p s t -> p (s t)")
             )
 
         def second_layer(acc, e, g):
+            key, i = (2, 0) if e == SHARED else divmod(e, 2)
+            cols = slice(i * N, (i + 1) * N)
             nc.tensor.matmul_mx(
                 out=acc,
-                lhsT=codes["w2", e][:].bitcast(FP8X4),
-                lhsT_scale=scales["w2", e][:],
-                rhs=h_codes[e, g][:].bitcast(FP8X4),
-                rhs_scale=h_scales[e, g][:],
+                lhsT=codes["w2", key][:, cols].bitcast(FP8X4),
+                lhsT_scale=scales["w2", key][:, cols],
+                rhs=h_codes[e, g].bitcast(FP8X4),
+                rhs_scale=h_scales[e, g],
                 start=True,
                 stop=True,
             )
-
-        S1 = {SHARED: 96, 0: 96, 1: 96, 2: 96, 3: 96}
-        S3 = {SHARED: 56, 0: 72, 1: 72, 2: 72, 3: 64}
-
-        def prepare_first(e):
-            new_weight("w1", e)
-            cast_hidden(nc.scalar.copy, "w1", e, 0, S1[e])
-            cast_hidden(nc.vector.tensor_copy, "w1", e, S1[e], P)
-
-        def prepare_second(e):
-            new_weight("w3", e)
-            cast_hidden(nc.scalar.copy, "w3", e, 0, S3[e])
-            cast_hidden(nc.vector.tensor_copy, "w3", e, S3[e], P)
-
-        def prepare_out(e, engine):
-            new_weight("w2", e)
-            cast_out(engine, e)
 
         shared_acc = psum.tile([P, T], F32, name="shared_acc")
         result = keep.tile([P, T], F32, name="result")
@@ -184,74 +208,115 @@ def tile_moe_shr_glu_gelu_kernel(tc, xT, w1, w3, w2, gate, offs, out):
         def shared_out(g):
             second_layer(shared_acc[:, g * C : (g + 1) * C], SHARED, g)
 
+        def new_routed(*experts):
+            acc = psum.tile([P, len(experts) * C], F32, name="routed_acc", bufs=2)
+            for i, e in enumerate(experts):
+                routed_acc[e] = acc, i
+
         def route(e):
-            routed_acc[e] = psum.tile([P, C], F32, name="routed_acc", bufs=2)
-            second_layer(routed_acc[e][:], e, e)
+            acc, i = routed_acc[e]
+            second_layer(acc[:, i * C : (i + 1) * C], e, e)
 
-        def weigh(e):
-            weighted[e] = work.tile([P, C], F32, name="weighted")
-            nc.vector.tensor_tensor(weighted[e][:], routed_acc[e][:], gates[:, e * C : (e + 1) * C], MULT)
+        def weigh(lo, hi):
+            weighted[lo] = work.tile([P, (hi - lo) * C], F32, name="weighted")
+            nc.vector.tensor_tensor(weighted[lo][:], routed_acc[lo][0][:], gates[:, lo * C : hi * C], MULT)
 
-        def add_shared(e):
-            total[e] = work.tile([P, C], F32, name="total")
-            nc.vector.tensor_tensor(total[e][:], weighted[e][:], shared_acc[:, e * C : (e + 1) * C], ADD)
+        def add_shared(lo, hi):
+            total[lo] = work.tile([P, (hi - lo) * C], F32, name="total")
+            nc.vector.tensor_tensor(total[lo][:], weighted[lo][:], shared_acc[:, lo * C : hi * C], ADD)
 
-        def scatter(e):
+        def scatter(lo, hi):
             nc.vector.tensor_copy(
-                result[:].indirect(offsets[:, e * C // 16 : (e + 1) * C // 16]), total[e][:]
+                result[:].indirect(offsets[:, lo * C // 16 : hi * C // 16]), total[lo][:]
             )
 
-        prepare_first(SHARED)
+        new_gelu(*[(SHARED, g) for g in range(E)], tag="gelu_shared")
+        prepare("w1", SHARED)
         quantize_weight("w1", SHARED)
-        prepare_second(SHARED)
-        first_layer_gelu(SHARED, 0)
-        first_layer_gelu(SHARED, 1)
-        first_layer_gelu(SHARED, 2)
+        mm_gelu(SHARED, 0)
+        prepare("w3", SHARED)
+        mm_gelu(SHARED, 1)
+        apply_gelu(SHARED, 0)
+        prepare_out(nc.vector.tensor_copy, 2)
         quantize_weight("w3", SHARED)
-        first_layer_linear(SHARED, 0)
-        first_layer_linear(SHARED, 1)
-        prepare_out(SHARED, nc.vector.tensor_copy)
+        quantize_weight("w2", 2)
+        mm_linear(SHARED, 0)
+        mm_gelu(SHARED, 2)
+        mm_linear(SHARED, 1)
+        apply_gelu(SHARED, 1)
+        h_front = new_hidden((SHARED, 0), (SHARED, 1))
+        h_back = new_hidden((SHARED, 2), (SHARED, 3))
         gate_hidden(SHARED, 0)
-        first_layer_linear(SHARED, 2)
-        prepare_first(0)
-        first_layer_gelu(SHARED, 3)
+        mm_linear(SHARED, 2)
+        apply_gelu(SHARED, 2)
+        mm_gelu(SHARED, 3)
+        prepare("w1", 0)
         gate_hidden(SHARED, 1)
-        first_layer_linear(SHARED, 3)
-        quantize_hidden(SHARED, 0)
-        quantize_weight("w2", SHARED)
+        apply_gelu(SHARED, 3)
+        mm_linear(SHARED, 3)
+        quantize_hidden(h_front)
         gate_hidden(SHARED, 2)
-        quantize_hidden(SHARED, 1)
+        quantize_weight("w1", 0)
+        mm_gelu(0, 0)
+        prepare("w3", 0)
         gate_hidden(SHARED, 3)
-        quantize_hidden(SHARED, 2)
-        shared_out(0)
-        shared_out(1)
-        shared_out(2)
+        quantize_hidden(h_back)
+        for g in range(E):
+            shared_out(g)
+        quantize_weight("w3", 0)
+        mm_linear(0, 0)
 
-        for e in range(E):
-            last = (e - 1, e - 1) if e else (SHARED, E - 1)
-            quantize_weight("w1", e)
-            quantize_hidden(*last)
-            prepare_second(e)
-            first_layer_gelu(e, e)
-            if e:
-                route(e - 1)
-                weigh(e - 1)
-            else:
-                shared_out(E - 1)
-            prepare_out(e, nc.scalar.copy)
-            quantize_weight("w3", e)
-            first_layer_linear(e, e)
-            if e:
-                add_shared(e - 1)
-            if e < E - 1:
-                prepare_first(e + 1)
-            quantize_weight("w2", e)
-            gate_hidden(e, e)
-            if e:
-                scatter(e - 1)
-        quantize_hidden(E - 1, E - 1)
-        route(E - 1)
-        weigh(E - 1)
-        add_shared(E - 1)
-        scatter(E - 1)
+        prepare("w1", 1)
+        quantize_weight("w1", 1)
+        mm_gelu(1, 1)
+        prepare("w3", 1)
+        quantize_weight("w3", 1)
+        mm_linear(1, 1)
+        prepare_out(nc.vector.tensor_copy, 0)
+        quantize_weight("w2", 0)
+        new_gelu((0, 0), (1, 1), tag="w3_raw1")
+        apply_gelu(0, 0)
+        apply_gelu(1, 1)
+        h = [new_hidden((e, e)) for e in range(2)]
+        gate_hidden(0, 0)
+        gate_hidden(1, 1)
+        quantize_hidden(h[0])
+        quantize_hidden(h[1])
+        new_routed(0, 1)
+        route(0)
+        route(1)
+        weigh(0, 2)
+        add_shared(0, 2)
+        prepare("w1", 2)
+        quantize_weight("w1", 2)
+        mm_gelu(2, 2)
+        scatter(0, 2)
+        prepare("w3", 2)
+        quantize_weight("w3", 2)
+        mm_linear(2, 2)
+        prepare("w1", 3)
+        quantize_weight("w1", 3)
+        mm_gelu(3, 3)
+        prepare("w3", 3)
+        quantize_weight("w3", 3)
+        mm_linear(3, 3)
+        new_gelu((2, 2), (3, 3), tag="w3_raw3")
+        apply_gelu(2, 2)
+        apply_gelu(3, 3)
+        prepare_out(nc.vector.tensor_copy, 1)
+        quantize_weight("w2", 1)
+        h = [new_hidden((e, e)) for e in (2, 3)]
+        gate_hidden(2, 2)
+        gate_hidden(3, 3)
+        quantize_hidden(h[0])
+        quantize_hidden(h[1])
+        for e in (2, 3):
+            new_routed(e)
+            route(e)
+        weigh(2, 3)
+        add_shared(2, 3)
+        weigh(3, 4)
+        scatter(2, 3)
+        add_shared(3, 4)
+        scatter(3, 4)
         nc.sync.dma_start(out, result[:])

@@ -38,7 +38,7 @@ def tile_moe_shr_glu_gelu_kernel(tc, xT, w1, w3, w2, gate, offs, out):
         w_raw = {}
 
         def load(name, src, e):
-            raw = keep.tile([P, PACK, src.shape[2]], F32, name=f"{name}_raw{e}", tag=f"{name}_raw{e}")
+            raw = keep.tile([P, PACK, src.shape[2]], F32, name=f"{name}_raw{e}", tag=f"{name}_raw{e}", align_bytes=64)
             nc.sync.dma_start(raw[:], src[e].rearrange("(p j) c -> p j c", j=PACK))
             w_raw[name, e] = raw
 
@@ -51,15 +51,15 @@ def tile_moe_shr_glu_gelu_kernel(tc, xT, w1, w3, w2, gate, offs, out):
         gates = keep.tile([P, T], F32, name="gates")
         load("w1", w1, SHARED)
         load("w3", w3, SHARED)
-        load("w1", w1, 0)
         load_w2(2, SHARED, SHARED + 1)
+        load("w1", w1, 0)
         load("w3", w3, 0)
+        load_w2(0, 0, 2)
         load("w1", w1, 1)
         load("w3", w3, 1)
-        load_w2(0, 0, 2)
-        nc.sync.dma_start(gates[:], gate)
         load("w1", w1, 2)
         load("w3", w3, 2)
+        nc.sync.dma_start(gates[:], gate)
         load("w1", w1, 3)
         load("w3", w3, 3)
         load_w2(1, 2, 4)
@@ -93,8 +93,8 @@ def tile_moe_shr_glu_gelu_kernel(tc, xT, w1, w3, w2, gate, offs, out):
         codes = {}
         scales = {}
         grouped = {}
-        S1 = {SHARED: 96, 0: 80, 1: 80, 2: 80, 3: 88}
-        S3 = {SHARED: 64, 0: 88, 1: 88, 2: 88, 3: 72}
+        S1 = {SHARED: 104, 0: 48, 1: 88, 2: 88, 3: 96}
+        S3 = {SHARED: 96, 0: 56, 1: 80, 2: 96, 3: 56}
 
         def new_weight(name, e, width):
             grouped[name, e] = keep.tile([P, width * PACK], BF16, name=f"{name}_grouped{e}", align_bytes=64)
@@ -153,7 +153,7 @@ def tile_moe_shr_glu_gelu_kernel(tc, xT, w1, w3, w2, gate, offs, out):
             hidden_product(gelu_in[e, g], "w1", e, g)
 
         def new_gelu(*units, tag):
-            tile = keep.tile([P, len(units) * C, PACK], F32, name=f"gelu_{tag}", tag=tag)
+            tile = keep.tile([P, len(units) * C, PACK], F32, name=f"gelu_{tag}", tag=tag, align_bytes=64)
             for i, unit in enumerate(units):
                 gelus[unit] = tile[:, i * C : (i + 1) * C]
 
@@ -164,37 +164,40 @@ def tile_moe_shr_glu_gelu_kernel(tc, xT, w1, w3, w2, gate, offs, out):
             linear[e, g] = psum.tile([P, PACK, C], F32, name="linear_acc", bufs=2)
             hidden_product(linear[e, g], "w3", e, g)
 
-        def new_hidden(*units):
-            width = len(units) * C
-            tile = work.tile([P, width, PACK], BF16, name="gated", align_bytes=64)
-            c = work.tile([P, width], U32, name="h_codes", align_bytes=64)
-            s = work.tile([P, width], U8, name="h_scales", align_bytes=64)
-            for i, unit in enumerate(units):
-                gated[unit] = tile[:, i * C : (i + 1) * C]
-                h_codes[unit] = c[:, i * C : (i + 1) * C]
-                h_scales[unit] = s[:, i * C : (i + 1) * C]
-            return tile, c, s
+        def new_hidden(e, lo, hi, tag=None):
+            label = f"{e}_{lo}"
+            tag = tag or f"gated{label}"
+            gated[e, lo] = keep.tile([P, hi - lo, PACK], BF16, name=f"gated{label}", tag=tag, align_bytes=64)
+            h_codes[e, lo] = keep.tile([P, hi - lo], U32, name=f"h_codes{label}", align_bytes=64)
+            h_scales[e, lo] = keep.tile([P, hi - lo], U8, name=f"h_scales{label}", align_bytes=64)
 
-        def gate_hidden(e, g):
+        def gate_hidden(e, base, lo, hi):
+            g = lo // C
+            here = slice(lo - g * C, hi - g * C)
             nc.vector.tensor_tensor(
-                gated[e, g], gelus[e, g], linear[e, g][:].rearrange("p t s -> p s t"), MULT
+                gated[e, base][:, lo - base : hi - base],
+                gelus[e, g][:, here],
+                linear[e, g][:, :, here].rearrange("p t s -> p s t"),
+                MULT,
             )
 
-        def quantize_hidden(h):
-            tile, c, s = h
+        def quantize_hidden(e, base):
             nc.vector.quantize_mx(
-                out=c[:].bitcast(FP8X4), scales=s[:], in_=tile[:].rearrange("p s t -> p (s t)")
+                out=h_codes[e, base][:].bitcast(FP8X4),
+                scales=h_scales[e, base][:],
+                in_=gated[e, base][:].rearrange("p s t -> p (s t)"),
             )
 
-        def second_layer(acc, e, g):
+        def second_layer(acc, e, base, lo, hi):
             key, i = (2, 0) if e == SHARED else divmod(e, 2)
             cols = slice(i * N, (i + 1) * N)
+            slots = slice(lo - base, hi - base)
             nc.tensor.matmul_mx(
                 out=acc,
                 lhsT=codes["w2", key][:, cols].bitcast(FP8X4),
                 lhsT_scale=scales["w2", key][:, cols],
-                rhs=h_codes[e, g].bitcast(FP8X4),
-                rhs_scale=h_scales[e, g],
+                rhs=h_codes[e, base][:, slots].bitcast(FP8X4),
+                rhs_scale=h_scales[e, base][:, slots],
                 start=True,
                 stop=True,
             )
@@ -205,30 +208,28 @@ def tile_moe_shr_glu_gelu_kernel(tc, xT, w1, w3, w2, gate, offs, out):
         weighted = {}
         total = {}
 
-        def shared_out(g):
-            second_layer(shared_acc[:, g * C : (g + 1) * C], SHARED, g)
+        def shared_out(g, base):
+            lo = g * C
+            second_layer(shared_acc[:, lo : lo + C], SHARED, base, lo, lo + C)
 
-        def new_routed(*experts):
-            acc = psum.tile([P, len(experts) * C], F32, name="routed_acc", bufs=2)
-            for i, e in enumerate(experts):
-                routed_acc[e] = acc, i
+        def new_routed(lo, hi):
+            routed_acc[lo] = psum.tile([P, hi - lo], F32, name="routed_acc", bufs=2)
 
-        def route(e):
-            acc, i = routed_acc[e]
-            second_layer(acc[:, i * C : (i + 1) * C], e, e)
+        def route(base, e, lo, hi):
+            second_layer(routed_acc[base][:, lo - base : hi - base], e, lo, lo, hi)
 
-        def weigh(lo, hi):
-            weighted[lo] = work.tile([P, (hi - lo) * C], F32, name="weighted")
-            nc.vector.tensor_tensor(weighted[lo][:], routed_acc[lo][0][:], gates[:, lo * C : hi * C], MULT)
+        def weigh(base, lo, hi):
+            weighted[lo] = work.tile([P, hi - lo], F32, name="weighted")
+            nc.vector.tensor_tensor(
+                weighted[lo][:], routed_acc[base][:, lo - base : hi - base], gates[:, lo:hi], MULT
+            )
 
         def add_shared(lo, hi):
-            total[lo] = work.tile([P, (hi - lo) * C], F32, name="total")
-            nc.vector.tensor_tensor(total[lo][:], weighted[lo][:], shared_acc[:, lo * C : hi * C], ADD)
+            total[lo] = work.tile([P, hi - lo], F32, name="total")
+            nc.vector.tensor_tensor(total[lo][:], weighted[lo][:], shared_acc[:, lo:hi], ADD)
 
         def scatter(lo, hi):
-            nc.vector.tensor_copy(
-                result[:].indirect(offsets[:, lo * C // 16 : hi * C // 16]), total[lo][:]
-            )
+            nc.vector.tensor_copy(result[:].indirect(offsets[:, lo // 16 : hi // 16]), total[lo][:])
 
         new_gelu(*[(SHARED, g) for g in range(E)], tag="gelu_shared")
         prepare("w1", SHARED)
@@ -237,60 +238,65 @@ def tile_moe_shr_glu_gelu_kernel(tc, xT, w1, w3, w2, gate, offs, out):
         prepare("w3", SHARED)
         mm_gelu(SHARED, 1)
         apply_gelu(SHARED, 0)
-        prepare_out(nc.vector.tensor_copy, 2)
+        prepare_out(nc.scalar.copy, 2)
         quantize_weight("w3", SHARED)
         quantize_weight("w2", 2)
         mm_linear(SHARED, 0)
         mm_gelu(SHARED, 2)
         mm_linear(SHARED, 1)
         apply_gelu(SHARED, 1)
-        h_front = new_hidden((SHARED, 0), (SHARED, 1))
-        h_back = new_hidden((SHARED, 2), (SHARED, 3))
-        gate_hidden(SHARED, 0)
+        new_hidden(SHARED, 0, HALF)
+        new_hidden(SHARED, HALF, T)
+        gate_hidden(SHARED, 0, 0, C)
         mm_linear(SHARED, 2)
         apply_gelu(SHARED, 2)
         mm_gelu(SHARED, 3)
         prepare("w1", 0)
-        gate_hidden(SHARED, 1)
+        gate_hidden(SHARED, 0, C, 2 * C)
         apply_gelu(SHARED, 3)
         mm_linear(SHARED, 3)
-        quantize_hidden(h_front)
-        gate_hidden(SHARED, 2)
+        quantize_hidden(SHARED, 0)
+        gate_hidden(SHARED, HALF, 2 * C, 3 * C)
         quantize_weight("w1", 0)
         mm_gelu(0, 0)
         prepare("w3", 0)
-        gate_hidden(SHARED, 3)
-        quantize_hidden(h_back)
-        for g in range(E):
-            shared_out(g)
+        gate_hidden(SHARED, HALF, 3 * C, 4 * C)
+        quantize_hidden(SHARED, HALF)
+        shared_out(0, 0)
+        shared_out(1, 0)
         quantize_weight("w3", 0)
         mm_linear(0, 0)
-
+        shared_out(2, HALF)
+        shared_out(3, HALF)
+        prepare_out(nc.scalar.copy, 0)
         prepare("w1", 1)
         quantize_weight("w1", 1)
         mm_gelu(1, 1)
         prepare("w3", 1)
         quantize_weight("w3", 1)
         mm_linear(1, 1)
-        prepare_out(nc.vector.tensor_copy, 0)
         quantize_weight("w2", 0)
         new_gelu((0, 0), (1, 1), tag="w3_raw1")
         apply_gelu(0, 0)
         apply_gelu(1, 1)
-        h = [new_hidden((e, e)) for e in range(2)]
-        gate_hidden(0, 0)
-        gate_hidden(1, 1)
-        quantize_hidden(h[0])
-        quantize_hidden(h[1])
-        new_routed(0, 1)
-        route(0)
-        route(1)
-        weigh(0, 2)
-        add_shared(0, 2)
+        for e in (0, 1):
+            new_hidden(e, e * C, (e + 1) * C)
+            gate_hidden(e, e * C, e * C, (e + 1) * C)
+        for e in (0, 1):
+            quantize_hidden(e, e * C)
+        for e in (0, 1):
+            lo, hi = e * C, (e + 1) * C
+            new_routed(lo, hi)
+            route(lo, e, lo, hi)
+        for e in (0, 1):
+            weigh(e * C, e * C, (e + 1) * C)
+        for e in (0, 1):
+            add_shared(e * C, (e + 1) * C)
         prepare("w1", 2)
         quantize_weight("w1", 2)
         mm_gelu(2, 2)
-        scatter(0, 2)
+        for e in (0, 1):
+            scatter(e * C, (e + 1) * C)
         prepare("w3", 2)
         quantize_weight("w3", 2)
         mm_linear(2, 2)
@@ -300,23 +306,33 @@ def tile_moe_shr_glu_gelu_kernel(tc, xT, w1, w3, w2, gate, offs, out):
         prepare("w3", 3)
         quantize_weight("w3", 3)
         mm_linear(3, 3)
-        new_gelu((2, 2), (3, 3), tag="w3_raw3")
+        new_gelu((2, 2), (3, 3), tag="gelu_back")
         apply_gelu(2, 2)
         apply_gelu(3, 3)
-        prepare_out(nc.vector.tensor_copy, 1)
+        prepare_out(nc.scalar.copy, 1)
         quantize_weight("w2", 1)
-        h = [new_hidden((e, e)) for e in (2, 3)]
-        gate_hidden(2, 2)
-        gate_hidden(3, 3)
-        quantize_hidden(h[0])
-        quantize_hidden(h[1])
-        for e in (2, 3):
-            new_routed(e)
-            route(e)
-        weigh(2, 3)
-        add_shared(2, 3)
-        weigh(3, 4)
-        scatter(2, 3)
-        add_shared(3, 4)
-        scatter(3, 4)
+        new_hidden(2, 2 * C, 3 * C, tag="w3_raw3")
+        gate_hidden(2, 2 * C, 2 * C, 3 * C)
+        STEP = C // 1
+        ends = [(lo, lo + STEP) for lo in range(3 * C, 4 * C, STEP)]
+        for lo, hi in ends:
+            new_hidden(3, lo, hi)
+            gate_hidden(3, lo, lo, hi)
+        quantize_hidden(2, 2 * C)
+        for lo, hi in ends:
+            quantize_hidden(3, lo)
+        new_routed(2 * C, 3 * C)
+        new_routed(3 * C, 4 * C)
+        route(2 * C, 2, 2 * C, 3 * C)
+        for lo, hi in ends:
+            route(3 * C, 3, lo, hi)
+        weigh(2 * C, 2 * C, 3 * C)
+        add_shared(2 * C, 3 * C)
+        for lo, hi in ends:
+            weigh(3 * C, lo, hi)
+        scatter(2 * C, 3 * C)
+        for lo, hi in ends:
+            add_shared(lo, hi)
+        for lo, hi in ends:
+            scatter(lo, hi)
         nc.sync.dma_start(out, result[:])

from contextlib import ExitStack

import concourse.mybir as mybir

K, T, E, C, H, N = 512, 512, 4, 128, 512, 128
FLOPS = 2 * (2 * T) * (2 * K * H + H * N)

F32 = mybir.dt.float32
BF16 = mybir.dt.bfloat16
U32 = mybir.dt.uint32
U16 = mybir.dt.uint16
U8 = mybir.dt.uint8
FP8X4 = mybir.dt.float8_e4m3fn_x4
GELU = mybir.ActivationFunctionType.Gelu_apprx_tanh
MULT = mybir.AluOpType.mult
ADD = mybir.AluOpType.add

P = 128
PACK = 4
SHARED = E
HALF = T // 2


def tile_moe_shr_glu_gelu_kernel(tc, xT, w1, w3, w2, gate, offs, out):
    nc = tc.nc
    with ExitStack() as ctx:
        keep = ctx.enter_context(tc.tile_pool(name="keep", bufs=1))
        work = ctx.enter_context(tc.tile_pool(name="work", bufs=4))
        psum = ctx.enter_context(tc.psum_pool(name="psum", bufs=1))

        offsets = keep.tile([P, T // 16], U16, name="offsets")
        x_raw = [keep.tile([P, 2, T], F32, name=f"x_raw{u}") for u in range(2)]
        x_rows = xT.rearrange("(p u h) t -> p u h t", u=2, h=2)
        nc.sync.dma_start(x_raw[0][:], x_rows[:, 0])
        nc.sync.dma_start(offsets[:], offs)
        nc.sync.dma_start(x_raw[1][:], x_rows[:, 1])

        w_raw = {}

        def load(name, src, e):
            raw = keep.tile([P, PACK, src.shape[2]], F32, name=f"{name}_raw{e}", tag=f"{name}_raw{e}", align_bytes=64)
            nc.sync.dma_start(raw[:], src[e].rearrange("(p j) c -> p j c", j=PACK))
            w_raw[name, e] = raw

        w2_raw = {}

        def load_w2(key, lo, hi):
            w2_raw[key] = keep.tile([P, hi - lo, PACK * N], F32, name=f"w2_raw{key}")
            nc.sync.dma_start(w2_raw[key][:], w2[lo:hi].rearrange("e (p j) n -> p e (j n)", j=PACK))

        gates = keep.tile([P, T], F32, name="gates")
        load("w1", w1, SHARED)
        load("w3", w3, SHARED)
        load_w2(2, SHARED, SHARED + 1)
        load("w1", w1, 0)
        load("w3", w3, 0)
        load_w2(0, 0, 2)
        load("w1", w1, 1)
        load("w3", w3, 1)
        load("w1", w1, 2)
        load("w3", w3, 2)
        nc.sync.dma_start(gates[:], gate)
        load("w1", w1, 3)
        load("w3", w3, 3)
        load_w2(1, 2, 4)

        tiny = keep.tile([P, 2], F32, name="tiny")
        nc.gpsimd.memset(tiny[:], 0.0)
        nc.scalar.activation(tiny[:, 1:2], tiny[:, 0:1], GELU)

        x_pairs = [keep.tile([P, T, 2], BF16, name=f"x_pairs{u}", align_bytes=64) for u in range(2)]
        x_slots = keep.tile([P, T, PACK], BF16, name="x_slots", align_bytes=64)
        x_words = x_slots[:].rearrange("p s j -> p (s j)").bitcast(U32).rearrange("p (s u) -> p s u", u=2)
        x_codes = keep.tile([P, T], U32, name="x_codes", align_bytes=64)
        x_scales = keep.tile([P, T], U8, name="x_scales", align_bytes=64)
        XS = 0
        x_view = [r[:].rearrange("p h t -> p t h") for r in x_raw]
        nc.vector.tensor_copy(x_pairs[0][:, XS:], x_view[0][:, XS:])
        if XS:
            nc.scalar.copy(x_pairs[0][:, :XS], x_view[0][:, :XS])
        nc.scalar.copy(x_pairs[1][:], x_view[1])
        for u in range(2):
            window = x_pairs[u][:].rearrange("p t h -> p (t h)").bitcast(U32)
            for s in range(2):
                nc.vector.tensor_copy(
                    x_words[:, s * HALF : (s + 1) * HALF, u],
                    window.indirect(offsets[:, s * HALF // 16 : (s + 1) * HALF // 16]),
                )
        nc.vector.quantize_mx(
            out=x_codes[:].bitcast(FP8X4), scales=x_scales[:], in_=x_slots[:].rearrange("p s j -> p (s j)")
        )

        codes = {}
        scales = {}
        grouped = {}
        S1 = {SHARED: 104, 0: 48, 1: 88, 2: 88, 3: 96}
        S3 = {SHARED: 96, 0: 56, 1: 80, 2: 96, 3: 56}

        def new_weight(name, e, width):
            grouped[name, e] = keep.tile([P, width * PACK], BF16, name=f"{name}_grouped{e}", align_bytes=64)
            codes[name, e] = keep.tile([P, width], U32, name=f"{name}_codes{e}", align_bytes=64)
            scales[name, e] = keep.tile([P, width], U8, name=f"{name}_scales{e}", align_bytes=64)

        def cast_hidden(engine, name, e, lo, hi):
            if lo == hi:
                return
            dst = grouped[name, e][:].rearrange("p (t m j) -> p m j t", t=PACK, j=PACK)
            src = w_raw[name, e][:].rearrange("p j (m t) -> p m j t", t=PACK)
            engine(dst[:, lo:hi], src[:, lo:hi])

        def prepare(name, e):
            new_weight(name, e, H)
            split = (S1 if name == "w1" else S3)[e]
            cast_hidden(nc.scalar.copy, name, e, 0, split)
            cast_hidden(nc.vector.tensor_copy, name, e, split, P)

        def prepare_out(engine, key):
            width = w2_raw[key].shape[1] * N
            new_weight("w2", key, width)
            engine(
                grouped["w2", key][:].rearrange("p (e n j) -> p e n j", n=N, j=PACK),
                w2_raw[key][:].rearrange("p e (j n) -> p e n j", j=PACK),
            )

        def quantize_weight(name, e):
            nc.vector.quantize_mx(
                out=codes[name, e][:].bitcast(FP8X4), scales=scales[name, e][:], in_=grouped[name, e][:]
            )

        gelu_in = {}
        gelus = {}
        linear = {}
        gated = {}
        h_codes = {}
        h_scales = {}

        def hidden_product(acc, name, e, g):
            for t in range(PACK):
                cols = slice(t * P, (t + 1) * P)
                slots = slice(g * C, (g + 1) * C)
                nc.tensor.matmul_mx(
                    out=acc[:, t, :],
                    lhsT=codes[name, e][:, cols].bitcast(FP8X4),
                    lhsT_scale=scales[name, e][:, cols],
                    rhs=x_codes[:, slots].bitcast(FP8X4),
                    rhs_scale=x_scales[:, slots],
                    start=True,
                    stop=True,
                )

        def mm_gelu(e, g):
            gelu_in[e, g] = psum.tile([P, PACK, C], F32, name="gelu_acc", bufs=3)
            hidden_product(gelu_in[e, g], "w1", e, g)

        def new_gelu(*units, tag):
            tile = keep.tile([P, len(units) * C, PACK], F32, name=f"gelu_{tag}", tag=tag, align_bytes=64)
            for i, unit in enumerate(units):
                gelus[unit] = tile[:, i * C : (i + 1) * C]

        def apply_gelu(e, g):
            nc.scalar.activation(gelus[e, g], gelu_in[e, g][:].rearrange("p t s -> p s t"), GELU)

        def mm_linear(e, g):
            linear[e, g] = psum.tile([P, PACK, C], F32, name="linear_acc", bufs=2)
            hidden_product(linear[e, g], "w3", e, g)

        def new_hidden(e, lo, hi, tag=None):
            label = f"{e}_{lo}"
            tag = tag or f"gated{label}"
            gated[e, lo] = keep.tile([P, hi - lo, PACK], BF16, name=f"gated{label}", tag=tag, align_bytes=64)
            h_codes[e, lo] = keep.tile([P, hi - lo], U32, name=f"h_codes{label}", align_bytes=64)
            h_scales[e, lo] = keep.tile([P, hi - lo], U8, name=f"h_scales{label}", align_bytes=64)

        def gate_hidden(e, base, lo, hi):
            g = lo // C
            here = slice(lo - g * C, hi - g * C)
            nc.vector.tensor_tensor(
                gated[e, base][:, lo - base : hi - base],
                gelus[e, g][:, here],
                linear[e, g][:, :, here].rearrange("p t s -> p s t"),
                MULT,
            )

        def quantize_hidden(e, base):
            nc.vector.quantize_mx(
                out=h_codes[e, base][:].bitcast(FP8X4),
                scales=h_scales[e, base][:],
                in_=gated[e, base][:].rearrange("p s t -> p (s t)"),
            )

        def second_layer(acc, e, base, lo, hi):
            key, i = (2, 0) if e == SHARED else divmod(e, 2)
            cols = slice(i * N, (i + 1) * N)
            slots = slice(lo - base, hi - base)
            nc.tensor.matmul_mx(
                out=acc,
                lhsT=codes["w2", key][:, cols].bitcast(FP8X4),
                lhsT_scale=scales["w2", key][:, cols],
                rhs=h_codes[e, base][:, slots].bitcast(FP8X4),
                rhs_scale=h_scales[e, base][:, slots],
                start=True,
                stop=True,
            )

        shared_acc = psum.tile([P, T], F32, name="shared_acc")
        result = keep.tile([P, T], F32, name="result")
        routed_acc = {}
        weighted = {}
        total = {}

        def shared_out(g, base):
            lo = g * C
            second_layer(shared_acc[:, lo : lo + C], SHARED, base, lo, lo + C)

        def new_routed(lo, hi):
            routed_acc[lo] = psum.tile([P, hi - lo], F32, name="routed_acc", bufs=2)

        def route(base, e, lo, hi):
            second_layer(routed_acc[base][:, lo - base : hi - base], e, lo, lo, hi)

        def weigh(base, lo, hi):
            weighted[lo] = work.tile([P, hi - lo], F32, name="weighted")
            nc.vector.tensor_tensor(
                weighted[lo][:], routed_acc[base][:, lo - base : hi - base], gates[:, lo:hi], MULT
            )

        def add_shared(lo, hi):
            total[lo] = work.tile([P, hi - lo], F32, name="total")
            nc.vector.tensor_tensor(total[lo][:], weighted[lo][:], shared_acc[:, lo:hi], ADD)

        def scatter(lo, hi):
            nc.vector.tensor_copy(result[:].indirect(offsets[:, lo // 16 : hi // 16]), total[lo][:])

        new_gelu(*[(SHARED, g) for g in range(E)], tag="gelu_shared")
        prepare("w1", SHARED)
        quantize_weight("w1", SHARED)
        mm_gelu(SHARED, 0)
        prepare("w3", SHARED)
        mm_gelu(SHARED, 1)
        apply_gelu(SHARED, 0)
        prepare_out(nc.scalar.copy, 2)
        quantize_weight("w3", SHARED)
        quantize_weight("w2", 2)
        mm_linear(SHARED, 0)
        mm_gelu(SHARED, 2)
        mm_linear(SHARED, 1)
        apply_gelu(SHARED, 1)
        new_hidden(SHARED, 0, HALF)
        new_hidden(SHARED, HALF, T)
        gate_hidden(SHARED, 0, 0, C)
        mm_linear(SHARED, 2)
        apply_gelu(SHARED, 2)
        mm_gelu(SHARED, 3)
        prepare("w1", 0)
        gate_hidden(SHARED, 0, C, 2 * C)
        apply_gelu(SHARED, 3)
        mm_linear(SHARED, 3)
        quantize_hidden(SHARED, 0)
        gate_hidden(SHARED, HALF, 2 * C, 3 * C)
        quantize_weight("w1", 0)
        mm_gelu(0, 0)
        prepare("w3", 0)
        gate_hidden(SHARED, HALF, 3 * C, 4 * C)
        quantize_hidden(SHARED, HALF)
        shared_out(0, 0)
        shared_out(1, 0)
        quantize_weight("w3", 0)
        mm_linear(0, 0)
        shared_out(2, HALF)
        shared_out(3, HALF)
        prepare_out(nc.scalar.copy, 0)
        prepare("w1", 1)
        quantize_weight("w1", 1)
        mm_gelu(1, 1)
        prepare("w3", 1)
        quantize_weight("w3", 1)
        mm_linear(1, 1)
        quantize_weight("w2", 0)
        new_gelu((0, 0), (1, 1), tag="w3_raw1")
        apply_gelu(0, 0)
        apply_gelu(1, 1)
        for e in (0, 1):
            new_hidden(e, e * C, (e + 1) * C)
            gate_hidden(e, e * C, e * C, (e + 1) * C)
        for e in (0, 1):
            quantize_hidden(e, e * C)
        for e in (0, 1):
            lo, hi = e * C, (e + 1) * C
            new_routed(lo, hi)
            route(lo, e, lo, hi)
        for e in (0, 1):
            weigh(e * C, e * C, (e + 1) * C)
        for e in (0, 1):
            add_shared(e * C, (e + 1) * C)
        prepare("w1", 2)
        quantize_weight("w1", 2)
        mm_gelu(2, 2)
        for e in (0, 1):
            scatter(e * C, (e + 1) * C)
        prepare("w3", 2)
        quantize_weight("w3", 2)
        mm_linear(2, 2)
        prepare("w1", 3)
        quantize_weight("w1", 3)
        mm_gelu(3, 3)
        prepare("w3", 3)
        quantize_weight("w3", 3)
        mm_linear(3, 3)
        new_gelu((2, 2), (3, 3), tag="gelu_back")
        apply_gelu(2, 2)
        apply_gelu(3, 3)
        prepare_out(nc.scalar.copy, 1)
        quantize_weight("w2", 1)
        new_hidden(2, 2 * C, 3 * C, tag="w3_raw3")
        gate_hidden(2, 2 * C, 2 * C, 3 * C)
        STEP = C // 1
        ends = [(lo, lo + STEP) for lo in range(3 * C, 4 * C, STEP)]
        for lo, hi in ends:
            new_hidden(3, lo, hi)
            gate_hidden(3, lo, lo, hi)
        quantize_hidden(2, 2 * C)
        for lo, hi in ends:
            quantize_hidden(3, lo)
        new_routed(2 * C, 3 * C)
        new_routed(3 * C, 4 * C)
        route(2 * C, 2, 2 * C, 3 * C)
        for lo, hi in ends:
            route(3 * C, 3, lo, hi)
        weigh(2 * C, 2 * C, 3 * C)
        add_shared(2 * C, 3 * C)
        for lo, hi in ends:
            weigh(3 * C, lo, hi)
        scatter(2 * C, 3 * C)
        for lo, hi in ends:
            add_shared(lo, hi)
        for lo, hi in ends:
            scatter(lo, hi)
        nc.sync.dma_start(out, result[:])
